import numpy as np
import ml_dtypes


def mxq(x, axis, fmt="e4m3"):
    dtype, down = {"e4m3": (ml_dtypes.float8_e4m3fn, 7), "e5m2": (ml_dtypes.float8_e5m2, 14)}[fmt]
    v = np.moveaxis(np.asarray(x, np.float32).astype(ml_dtypes.bfloat16).astype(np.float64), axis, -1)
    blocks = v.reshape(v.shape[:-1] + (-1, 32))
    amax = np.abs(blocks).max(-1, keepdims=True)
    byte = np.maximum(np.where(amax > 0, np.frexp(amax)[1] - 1 + 127, 0) - down, 1)
    scale = np.exp2(byte - 127.0)
    codes = (blocks / scale).astype(np.float32).astype(dtype).astype(np.float64)
    return np.moveaxis((codes * scale).reshape(v.shape), -1, axis)


WIDE = False


def mx_kscale(k):
    if not WIDE:
        return np.ones(k)
    levels = np.array([10, -10, 5, -5, 0])
    if k % 512:
        return np.exp2(np.random.permutation(np.resize(levels, k // 32))).repeat(32)
    a = np.empty((k // 512, 16))
    for p in range(k // 512):
        a[p, :8] = np.random.permutation(np.resize(levels, 8))
        for g in range(8):
            far = levels[np.abs(levels - a[p, g]) >= 10]
            a[p, g + 8] = far[np.random.randint(len(far))]
    return np.exp2(a.ravel()).repeat(32)


def f64(x):
    return np.asarray(x).astype(np.float64)


def striped(idx):
    return np.tile(idx.reshape(-1, 16).T, (8, 1)).astype(np.uint16)


def unstriped(offs):
    return offs[:16].T.reshape(-1).astype(np.int64)


def striped8(idx):
    return np.concatenate([x.reshape(-1, 16).T for x in idx]).astype(np.uint16)


def runs(offs, k):
    lists = np.stack([offs[16 * r : 16 * r + 16].T.reshape(-1) for r in range(8)]).astype(np.int64)
    return lists[np.arange(k) % 512 // 64]


def pack_weight(w):
    k, n = w.shape
    w = f64(np.asarray(w, np.float32).astype(ml_dtypes.bfloat16)).reshape(k // 32, 32, n)
    amax = np.abs(w).max(1)
    byte = np.clip(np.where(amax > 0, np.frexp(amax)[1] - 1 + 127 - 7, 1), 1, 254)
    scaled = (w * np.exp2(127.0 - byte)[:, None, :]).reshape(k, n).astype(np.float32)
    words = np.ascontiguousarray(scaled.reshape(k // 512, 128, 4, n).transpose(0, 1, 3, 2)).astype(ml_dtypes.float8_e4m3fn).view(np.uint8)
    return words, np.ascontiguousarray(byte.astype(np.uint8).reshape(k // 512, 16, n))


def unpack_weight(words, scales):
    g, p, n, _ = words.shape
    vals = np.ascontiguousarray(words).view(ml_dtypes.float8_e4m3fn).astype(np.float64) * np.repeat(np.exp2(scales.astype(np.float64) - 127.0), 8, axis=1)[..., None]
    return vals.transpose(0, 1, 3, 2).reshape(g * 512, n)


K, T, S, N, U, H = 512, 2048, 512, 512, 1024, 512


def setup_inputs():
    n = np.random.standard_normal
    s = mx_kscale(K)[:, None]
    u = mx_kscale(H)
    packed_xT = pack_weight(n((K, T)) * s)
    perm = np.stack([np.random.permutation(U) for _ in range(8)])
    return {
        "x_words": packed_xT[0],
        "x_scales": packed_xT[1],
        "w1": (n((K, H)) / np.sqrt(K) / s * u).astype(np.float32),
        "w2": (n((K, H)) / np.sqrt(K) / s * u).astype(np.float32),
        "w3": (n((H, N)) / np.sqrt(H) / u[:, None]).astype(np.float32),
        "offs": striped(np.random.permutation(T)[:S]),
        "two": striped(np.random.permutation(T)[:S]),
        "la": striped8(perm[:, :S]),
        "lb": striped8(perm[:, S:]),
        "mate": striped8(np.stack([np.random.permutation(U) for _ in range(8)])),
    }


def reference(x_words, x_scales, w1, w2, w3, offs, two, la, lb, mate):
    x_two = unpack_weight(x_words, x_scales)[:, unstriped(two)]
    e = mxq(f64(w2), 0, "e4m3").T @ x_two
    xq = unpack_weight(x_words, x_scales)[:, unstriped(offs)]
    y = mxq(f64(w1), 0, "e4m3").T @ xq
    p = np.zeros((H, U))
    p[np.arange(H)[:, None], runs(la, H)] = y
    m1 = p.copy()
    m1[np.arange(H)[:, None], runs(lb, H)] = e
    z = np.maximum(m1, m1[np.arange(H)[:, None], runs(mate, H)])
    return mxq(f64(w3), 0, "e4m3").T @ mxq(z, 0, "e4m3")

@@ -1,0 +1,170 @@
+from contextlib import ExitStack
+
+import concourse.mybir as mybir
+
+F32 = mybir.dt.float32
+BF16 = mybir.dt.bfloat16
+I32 = mybir.dt.int32
+U32 = mybir.dt.uint32
+U16 = mybir.dt.uint16
+U8 = mybir.dt.uint8
+FP8X4 = mybir.dt.float8_e4m3fn_x4
+MAX = mybir.AluOpType.max
+
+K, T, S, N, U, H = 512, 2048, 512, 512, 1024, 512
+P = 128
+PACK = 4
+LIST_ROWS = 16
+FLOPS = 2 * K * H * S * 2 + 2 * H * N * U
+
+GATHER_SPANS = ((0, 512), (512, 768), (768, 1024))
+PIECES = (((0, 512),), ((512, 768),), ((768, 896), (896, 1024)))
+
+
+def tile_picked_mergemax_none_p_kernel(
+    tc, x_words, x_scales, w1, w2, w3, offs, two, la, lb, mate, out
+):
+    nc = tc.nc
+    with ExitStack() as ctx:
+        keep = ctx.enter_context(tc.tile_pool(name="keep", bufs=1))
+        ring = ctx.enter_context(tc.tile_pool(name="ring", bufs=2))
+        psum = ctx.enter_context(tc.psum_pool(name="psum", bufs=8))
+
+        def load_list(src, name):
+            lst = keep.tile(list(src.shape), U16, name=name)
+            nc.sync.dma_start(lst[:], src)
+            return lst
+
+        def load_weight(src, name):
+            raw = keep.tile([P, PACK, src.shape[1]], F32, name=name)
+            nc.sync.dma_start(raw[:], src.rearrange("(p j) c -> p j c", j=PACK))
+            return raw
+
+        table_scales = keep.tile([P, T], U8, name="table_scales")
+        nc.vector.memset(table_scales[:].bitcast(I32), 0)
+        table_words = keep.tile([P, T], I32, name="table_words")
+        words_hbm = x_words[0].rearrange("p n t -> p (n t)").bitcast(I32)
+
+        offs_t = load_list(offs, "offs_t")
+        two_t = load_list(two, "two_t")
+        nc.sync.dma_start(table_words[:, : T // 2], words_hbm[:, : T // 2])
+        for r in range(4):
+            nc.sync.dma_start(table_scales[r:P:32, :].bitcast(I32), x_scales[0, r:16:4, :].bitcast(I32))
+        nc.sync.dma_start(table_words[:, T // 2 :], words_hbm[:, T // 2 :])
+        w1_raw = load_weight(w1, "w1_raw")
+        la_t = load_list(la, "la_t")
+        w2_raw = load_weight(w2, "w2_raw")
+        lb_t = load_list(lb, "lb_t")
+        w3_raw = load_weight(w3, "w3_raw")
+        mate_t = load_list(mate, "mate_t")
+
+        def gather_scales(lst, name):
+            picked = keep.tile([P, S], U8, name=name, align_bytes=64)
+            nc.vector.tensor_copy(picked[:], table_scales[:].indirect(lst[:]))
+            return picked
+
+        def gather_words(lst, name, tag):
+            picked = keep.tile([P, S], U32, name=name, tag=tag, align_bytes=64)
+            nc.vector.tensor_copy(picked[:], table_words[:].bitcast(U32).indirect(lst[:]))
+            return picked
+
+        def deal_weight(copy, raw, half, name, tag):
+            dealt = keep.tile([P, 2, P, PACK], BF16, name=name, tag=tag, align_bytes=64)
+            copy(
+                dealt[:].rearrange("p t m j -> p m j t"),
+                raw[:].rearrange("p j (m t) -> p m j t", t=PACK)[:, :, :, 2 * half : 2 * half + 2],
+            )
+            return dealt[:].rearrange("p t m j -> p (t m j)")
+
+        def quantize(pool, values, name):
+            width = values.shape[1] // PACK
+            codes = pool.tile([P, width], U32, name=name + "_codes", align_bytes=64)
+            scales = pool.tile([P, width], U8, name=name + "_scales", align_bytes=64)
+            nc.vector.quantize_mx(out=codes[:].bitcast(FP8X4), scales=scales[:], in_=values)
+            return codes, scales
+
+        def product(dst, weights, col, moving):
+            nc.tensor.matmul_mx(
+                out=dst,
+                lhsT=weights[0][:, col : col + P].bitcast(FP8X4),
+                lhsT_scale=weights[1][:, col : col + P],
+                rhs=moving[0][:].bitcast(FP8X4),
+                rhs_scale=moving[1][:],
+                start=True,
+                stop=True,
+            )
+
+        def project(weights, moving, name):
+            tiles = []
+            for t in range(2):
+                bank = psum.tile([P, S], F32, name="bank")
+                product(bank[:], weights, t * P, moving)
+                res = keep.tile([P, S], F32, name=name + str(t))
+                nc.scalar.copy(res[:], bank[:])
+                tiles.append(res)
+            return tiles
+
+        offs_scales = gather_scales(offs_t, "offs_scales")
+        two_scales = gather_scales(two_t, "two_scales")
+        offs_words = gather_words(offs_t, "offs_words", "offs_words")
+        w1_lo = deal_weight(nc.vector.tensor_copy, w1_raw, 0, "w1_lo", "early")
+        w1_hi = deal_weight(nc.scalar.copy, w1_raw, 1, "w1_hi", "w1_hi")
+        w1_lo_q = quantize(keep, w1_lo, "w1_lo")
+        y = project(w1_lo_q, (offs_words, offs_scales), "y_lo")
+        two_words = gather_words(two_t, "two_words", "early")
+        y = y + project(quantize(keep, w1_hi, "w1_hi"), (offs_words, offs_scales), "y_hi")
+
+        merged = [keep.tile([P, U], F32, name="merged" + str(t)) for t in range(PACK)]
+        for t in range(PACK):
+            nc.vector.tensor_copy(merged[t][:].indirect(la_t[:]), y[t][:])
+
+        e = []
+        for half in range(2):
+            name = "w2_" + str(half)
+            dealt = deal_weight(nc.scalar.copy, w2_raw, half, name, name)
+            e = e + project(quantize(keep, dealt, name), (two_words, two_scales), "e" + name)
+
+        w3_bf = keep.tile([P, N * PACK], BF16, name="w3_bf", align_bytes=64)
+        nc.scalar.copy(
+            w3_bf[:].rearrange("p (c i j) -> p c j i", i=2, j=PACK),
+            w3_raw[:].rearrange("p j (c i) -> p c j i", i=2),
+        )
+        w3_q = quantize(keep, w3_bf[:], "w3")
+
+        joined = keep.tile([P, PACK, U], F32, name="joined")
+        for t in range(PACK):
+            nc.vector.tensor_copy(merged[t][:].indirect(lb_t[:]), e[t][:])
+            nc.scalar.copy(joined[:, t, :], merged[t][:])
+
+        out_view = out.rearrange("(b p) w -> p b w", p=P)
+        for (lo, hi), pieces in zip(GATHER_SPANS, PIECES):
+            mates = ring.tile([P, PACK, hi - lo], F32, name="mates")
+            for t in range(PACK):
+                nc.vector.tensor_copy(
+                    mates[:, t, :], merged[t][:].indirect(mate_t[:, lo // LIST_ROWS : hi // LIST_ROWS])
+                )
+            zs = []
+            for a, b in pieces:
+                z = ring.tile([P, (b - a) * PACK], BF16, name="z", align_bytes=64)
+                nc.vector.tensor_tensor(
+                    z[:].rearrange("p (c i t) -> p c t i", i=2, t=PACK),
+                    joined[:, :, a:b].rearrange("p t (c i) -> p c t i", i=2),
+                    mates[:, :, a - lo : b - lo].rearrange("p t (c i) -> p c t i", i=2),
+                    MAX,
+                )
+                zs.append(z)
+            for (a, b), z in zip(pieces, zs):
+                width = b - a
+                z_q = quantize(ring, z[:], "z")
+                per_bank = S // width
+                for first in range(0, PACK, per_bank):
+                    bank = psum.tile([P, S], F32, name="bank")
+                    for i in range(per_bank):
+                        product(bank[:, i * width : (i + 1) * width], w3_q, (first + i) * P, z_q)
+                    staged = ring.tile([P, S], F32, name="staged", bufs=4)
+                    copy = nc.vector.tensor_copy if b == U else nc.scalar.copy
+                    copy(staged[:], bank[:])
+                    nc.sync.dma_start(
+                        out_view[:, first : first + per_bank, a:b],
+                        staged[:].rearrange("p (b w) -> p b w", b=per_bank),
+                    )

@@ -17,8 +17,10 @@ PACK = 4
 LIST_ROWS = 16
 FLOPS = 2 * K * H * S * 2 + 2 * H * N * U
 
-GATHER_SPANS = ((0, 512), (512, 768), (768, 1024))
-PIECES = (((0, 512),), ((512, 768),), ((768, 896), (896, 1024)))
+STAGES = (
+    (((0, 768),), ((0, 512), (512, 768)), "w3_raw"),
+    (((768, 1024),), ((768, 896), (896, 1024)), "z0"),
+)
 
 
 def tile_picked_mergemax_none_p_kernel(
@@ -36,7 +38,7 @@ def tile_picked_mergemax_none_p_kernel(
             return lst
 
         def load_weight(src, name):
-            raw = keep.tile([P, PACK, src.shape[1]], F32, name=name)
+            raw = keep.tile([P, PACK, src.shape[1]], F32, name=name, tag=name, align_bytes=64)
             nc.sync.dma_start(raw[:], src.rearrange("(p j) c -> p j c", j=PACK))
             return raw
 
@@ -45,36 +47,39 @@ def tile_picked_mergemax_none_p_kernel(
         table_words = keep.tile([P, T], I32, name="table_words")
         words_hbm = x_words[0].rearrange("p n t -> p (n t)").bitcast(I32)
 
+        nc.sync.dma_start(table_words[:, : T // 4], words_hbm[:, : T // 4])
         offs_t = load_list(offs, "offs_t")
         two_t = load_list(two, "two_t")
-        nc.sync.dma_start(table_words[:, : T // 2], words_hbm[:, : T // 2])
         for r in range(4):
             nc.sync.dma_start(table_scales[r:P:32, :].bitcast(I32), x_scales[0, r:16:4, :].bitcast(I32))
-        nc.sync.dma_start(table_words[:, T // 2 :], words_hbm[:, T // 2 :])
+        nc.sync.dma_start(table_words[:, T // 4 :], words_hbm[:, T // 4 :])
         w1_raw = load_weight(w1, "w1_raw")
         la_t = load_list(la, "la_t")
         w2_raw = load_weight(w2, "w2_raw")
         lb_t = load_list(lb, "lb_t")
-        w3_raw = load_weight(w3, "w3_raw")
         mate_t = load_list(mate, "mate_t")
+        w3_raw = keep.tile([P, PACK, N], F32, name="w3_raw", tag="w3_raw", align_bytes=64)
+        w3_rows = w3.rearrange("(b t q) n -> q b t n", t=PACK, q=8)
+        for q in range(8):
+            nc.sync.dma_start(w3_raw[q:P:8], w3_rows[q])
 
         def gather_scales(lst, name):
             picked = keep.tile([P, S], U8, name=name, align_bytes=64)
             nc.vector.tensor_copy(picked[:], table_scales[:].indirect(lst[:]))
             return picked
 
-        def gather_words(lst, name, tag):
-            picked = keep.tile([P, S], U32, name=name, tag=tag, align_bytes=64)
-            nc.vector.tensor_copy(picked[:], table_words[:].bitcast(U32).indirect(lst[:]))
+        def gather_words(lst, lo, hi, name, tag):
+            picked = keep.tile([P, hi - lo], U32, name=name, tag=tag, align_bytes=64)
+            nc.vector.tensor_copy(
+                picked[:], table_words[:].bitcast(U32).indirect(lst[:, lo // LIST_ROWS : hi // LIST_ROWS])
+            )
             return picked
 
-        def deal_weight(copy, raw, half, name, tag):
-            dealt = keep.tile([P, 2, P, PACK], BF16, name=name, tag=tag, align_bytes=64)
+        def deal_weight(copy, dealt, raw, t):
             copy(
-                dealt[:].rearrange("p t m j -> p m j t"),
-                raw[:].rearrange("p j (m t) -> p m j t", t=PACK)[:, :, :, 2 * half : 2 * half + 2],
+                dealt.rearrange("p (b h i j) -> p b h j i", h=4, i=2, j=PACK),
+                raw[:].rearrange("p j (b t h i) -> p t b h j i", t=PACK, h=4, i=2)[:, t],
             )
-            return dealt[:].rearrange("p t m j -> p (t m j)")
 
         def quantize(pool, values, name):
             width = values.shape[1] // PACK
@@ -83,69 +88,90 @@ def tile_picked_mergemax_none_p_kernel(
             nc.vector.quantize_mx(out=codes[:].bitcast(FP8X4), scales=scales[:], in_=values)
             return codes, scales
 
-        def product(dst, weights, col, moving):
+        def product(dst, weights, col, words, scales):
             nc.tensor.matmul_mx(
                 out=dst,
                 lhsT=weights[0][:, col : col + P].bitcast(FP8X4),
                 lhsT_scale=weights[1][:, col : col + P],
-                rhs=moving[0][:].bitcast(FP8X4),
-                rhs_scale=moving[1][:],
+                rhs=words.bitcast(FP8X4),
+                rhs_scale=scales,
                 start=True,
                 stop=True,
             )
 
-        def project(weights, moving, name):
-            tiles = []
-            for t in range(2):
-                bank = psum.tile([P, S], F32, name="bank")
-                product(bank[:], weights, t * P, moving)
-                res = keep.tile([P, S], F32, name=name + str(t))
-                nc.scalar.copy(res[:], bank[:])
-                tiles.append(res)
-            return tiles
+        def project(weights, col, parts, name):
+            bank = psum.tile([P, S], F32, name="bank")
+            at = 0
+            for words, scales in parts:
+                product(bank[:, at : at + words.shape[1]], weights, col, words, scales)
+                at = at + words.shape[1]
+            res = keep.tile([P, at], F32, name=name)
+            nc.scalar.copy(res[:], bank[:, :at])
+            return res
+
+        def scatter(window, lst, values, lo, hi):
+            nc.vector.tensor_copy(window[:].indirect(lst[:, lo // LIST_ROWS : hi // LIST_ROWS]), values[:])
 
         offs_scales = gather_scales(offs_t, "offs_scales")
         two_scales = gather_scales(two_t, "two_scales")
-        offs_words = gather_words(offs_t, "offs_words", "offs_words")
-        w1_lo = deal_weight(nc.vector.tensor_copy, w1_raw, 0, "w1_lo", "early")
-        w1_hi = deal_weight(nc.scalar.copy, w1_raw, 1, "w1_hi", "w1_hi")
-        w1_lo_q = quantize(keep, w1_lo, "w1_lo")
-        y = project(w1_lo_q, (offs_words, offs_scales), "y_lo")
-        two_words = gather_words(two_t, "two_words", "early")
-        y = y + project(quantize(keep, w1_hi, "w1_hi"), (offs_words, offs_scales), "y_hi")
-
-        merged = [keep.tile([P, U], F32, name="merged" + str(t)) for t in range(PACK)]
+        half = S // 2
+        offs_words = gather_words(offs_t, 0, S, "offs_words", "offs_words")
+        two_lo = gather_words(two_t, 0, half, "two_lo", "two_lo")
+        w1_bf = []
         for t in range(PACK):
-            nc.vector.tensor_copy(merged[t][:].indirect(la_t[:]), y[t][:])
+            dealt = keep.tile([P, P * PACK], BF16, name="w1_bf", tag="w1_bf" + str(t), align_bytes=64)
+            deal_weight(nc.vector.tensor_copy if t < 2 else nc.scalar.copy, dealt[:], w1_raw, t)
+            w1_bf.append(dealt)
+        w1_q = [quantize(keep, w1_bf[t][:], "w1_" + str(t)) for t in range(2)]
+        two_hi = gather_words(two_t, half, S, "two_hi", "w1_bf0")
+        w1_q = w1_q + [quantize(keep, w1_bf[t][:], "w1_" + str(t)) for t in range(2, PACK)]
+        offs_all = [(offs_words[:], offs_scales[:])]
+        two_all = [(two_lo[:], two_scales[:, :half]), (two_hi[:], two_scales[:, half:])]
+        y0a = project(w1_q[0], 0, [(offs_words[:, :half], offs_scales[:, :half])], "y0a")
+        y1 = project(w1_q[1], 0, offs_all, "y1")
+        y0b = project(w1_q[0], 0, [(offs_words[:, half:], offs_scales[:, half:])], "y0b")
+        y2 = project(w1_q[2], 0, offs_all, "y2")
+        y3 = project(w1_q[3], 0, offs_all, "y3")
 
-        e = []
-        for half in range(2):
-            name = "w2_" + str(half)
-            dealt = deal_weight(nc.scalar.copy, w2_raw, half, name, name)
-            e = e + project(quantize(keep, dealt, name), (two_words, two_scales), "e" + name)
+        merged = [keep.tile([P, U], F32, name="merged" + str(t), align_bytes=64) for t in range(PACK - 1)]
+        scatter(merged[0], la_t, y0a, 0, S // 2)
+        scatter(merged[1], la_t, y1, 0, S)
+        scatter(merged[0], la_t, y0b, S // 2, S)
+        scatter(merged[2], la_t, y2, 0, S)
 
-        w3_bf = keep.tile([P, N * PACK], BF16, name="w3_bf", align_bytes=64)
+        w2_bf = keep.tile([P, H * PACK], BF16, name="w2_bf", align_bytes=64)
+        for t in range(PACK):
+            deal_weight(nc.scalar.copy, w2_bf[:, t * P * PACK : (t + 1) * P * PACK], w2_raw, t)
+        w2_q = quantize(keep, w2_bf[:], "w2")
+        merged.append(keep.tile([P, U], F32, name="merged3", tag="w2_raw", align_bytes=64))
+        scatter(merged[3], la_t, y3, 0, S)
+        e = [project(w2_q, t * P, two_all, "e" + str(t)) for t in range(PACK)]
+
+        w3_bf = keep.tile([P, N * PACK], BF16, name="w3_bf", tag="w3_bf", align_bytes=64)
         nc.scalar.copy(
             w3_bf[:].rearrange("p (c i j) -> p c j i", i=2, j=PACK),
             w3_raw[:].rearrange("p j (c i) -> p c j i", i=2),
         )
         w3_q = quantize(keep, w3_bf[:], "w3")
 
-        joined = keep.tile([P, PACK, U], F32, name="joined")
+        joined = keep.tile([P, PACK, U], F32, name="joined", tag="w3_bf", align_bytes=64)
         for t in range(PACK):
-            nc.vector.tensor_copy(merged[t][:].indirect(lb_t[:]), e[t][:])
+            scatter(merged[t], lb_t, e[t], 0, S)
             nc.scalar.copy(joined[:, t, :], merged[t][:])
 
         out_view = out.rearrange("(b p) w -> p b w", p=P)
-        for (lo, hi), pieces in zip(GATHER_SPANS, PIECES):
-            mates = ring.tile([P, PACK, hi - lo], F32, name="mates")
-            for t in range(PACK):
-                nc.vector.tensor_copy(
-                    mates[:, t, :], merged[t][:].indirect(mate_t[:, lo // LIST_ROWS : hi // LIST_ROWS])
-                )
+        for spans, pieces, slot in STAGES:
+            lo, hi = spans[0][0], spans[-1][1]
+            mates = keep.tile([P, PACK, hi - lo], F32, name="mates", tag=slot, align_bytes=64)
+            for a, b in spans:
+                for t in range(PACK):
+                    nc.vector.tensor_copy(
+                        mates[:, t, a - lo : b - lo],
+                        merged[t][:].indirect(mate_t[:, a // LIST_ROWS : b // LIST_ROWS]),
+                    )
             zs = []
             for a, b in pieces:
-                z = ring.tile([P, (b - a) * PACK], BF16, name="z", align_bytes=64)
+                z = keep.tile([P, (b - a) * PACK], BF16, name="z", tag="z" + str(a), align_bytes=64)
                 nc.vector.tensor_tensor(
                     z[:].rearrange("p (c i t) -> p c t i", i=2, t=PACK),
                     joined[:, :, a:b].rearrange("p t (c i) -> p c t i", i=2),
@@ -155,16 +181,16 @@ def tile_picked_mergemax_none_p_kernel(
                 zs.append(z)
             for (a, b), z in zip(pieces, zs):
                 width = b - a
-                z_q = quantize(ring, z[:], "z")
-                per_bank = S // width
-                for first in range(0, PACK, per_bank):
+                z_q = quantize(keep, z[:], "z" + str(a))
+                per_bank = 2 if b == U else S // width
+                for first_block in range(0, PACK, per_bank):
                     bank = psum.tile([P, S], F32, name="bank")
                     for i in range(per_bank):
-                        product(bank[:, i * width : (i + 1) * width], w3_q, (first + i) * P, z_q)
-                    staged = ring.tile([P, S], F32, name="staged", bufs=4)
-                    copy = nc.vector.tensor_copy if b == U else nc.scalar.copy
-                    copy(staged[:], bank[:])
+                        product(bank[:, i * width : (i + 1) * width], w3_q, (first_block + i) * P, z_q[0][:], z_q[1][:])
+                    staged = ring.tile([P, per_bank * width], F32, name="staged", bufs=9)
+                    copy = nc.vector.tensor_copy if b == U and first_block == 0 else nc.scalar.copy
+                    copy(staged[:], bank[:, : per_bank * width])
                     nc.sync.dma_start(
-                        out_view[:, first : first + per_bank, a:b],
+                        out_view[:, first_block : first_block + per_bank, a:b],
                         staged[:].rearrange("p (b w) -> p b w", b=per_bank),
                     )

from contextlib import ExitStack

import concourse.mybir as mybir

F32 = mybir.dt.float32
BF16 = mybir.dt.bfloat16
I32 = mybir.dt.int32
U32 = mybir.dt.uint32
U16 = mybir.dt.uint16
U8 = mybir.dt.uint8
FP8X4 = mybir.dt.float8_e4m3fn_x4
MAX = mybir.AluOpType.max

K, T, S, N, U, H = 512, 2048, 512, 512, 1024, 512
P = 128
PACK = 4
LIST_ROWS = 16
FLOPS = 2 * K * H * S * 2 + 2 * H * N * U

STAGES = (
    (((0, 768),), ((0, 512), (512, 768)), "w3_raw"),
    (((768, 1024),), ((768, 896), (896, 1024)), "z0"),
)


def tile_picked_mergemax_none_p_kernel(
    tc, x_words, x_scales, w1, w2, w3, offs, two, la, lb, mate, out
):
    nc = tc.nc
    with ExitStack() as ctx:
        keep = ctx.enter_context(tc.tile_pool(name="keep", bufs=1))
        ring = ctx.enter_context(tc.tile_pool(name="ring", bufs=2))
        psum = ctx.enter_context(tc.psum_pool(name="psum", bufs=8))

        def load_list(src, name):
            lst = keep.tile(list(src.shape), U16, name=name)
            nc.sync.dma_start(lst[:], src)
            return lst

        def load_weight(src, name):
            raw = keep.tile([P, PACK, src.shape[1]], F32, name=name, tag=name, align_bytes=64)
            nc.sync.dma_start(raw[:], src.rearrange("(p j) c -> p j c", j=PACK))
            return raw

        table_scales = keep.tile([P, T], U8, name="table_scales")
        nc.vector.memset(table_scales[:].bitcast(I32), 0)
        table_words = keep.tile([P, T], I32, name="table_words")
        words_hbm = x_words[0].rearrange("p n t -> p (n t)").bitcast(I32)

        nc.sync.dma_start(table_words[:, : T // 4], words_hbm[:, : T // 4])
        offs_t = load_list(offs, "offs_t")
        two_t = load_list(two, "two_t")
        for r in range(4):
            nc.sync.dma_start(table_scales[r:P:32, :].bitcast(I32), x_scales[0, r:16:4, :].bitcast(I32))
        nc.sync.dma_start(table_words[:, T // 4 :], words_hbm[:, T // 4 :])
        w1_raw = load_weight(w1, "w1_raw")
        la_t = load_list(la, "la_t")
        w2_raw = load_weight(w2, "w2_raw")
        lb_t = load_list(lb, "lb_t")
        mate_t = load_list(mate, "mate_t")
        w3_raw = keep.tile([P, PACK, N], F32, name="w3_raw", tag="w3_raw", align_bytes=64)
        w3_rows = w3.rearrange("(b t q) n -> q b t n", t=PACK, q=8)
        for q in range(8):
            nc.sync.dma_start(w3_raw[q:P:8], w3_rows[q])

        def gather_scales(lst, name):
            picked = keep.tile([P, S], U8, name=name, align_bytes=64)
            nc.vector.tensor_copy(picked[:], table_scales[:].indirect(lst[:]))
            return picked

        def gather_words(lst, lo, hi, name, tag):
            picked = keep.tile([P, hi - lo], U32, name=name, tag=tag, align_bytes=64)
            nc.vector.tensor_copy(
                picked[:], table_words[:].bitcast(U32).indirect(lst[:, lo // LIST_ROWS : hi // LIST_ROWS])
            )
            return picked

        def deal_weight(copy, dealt, raw, t):
            copy(
                dealt.rearrange("p (b h i j) -> p b h j i", h=4, i=2, j=PACK),
                raw[:].rearrange("p j (b t h i) -> p t b h j i", t=PACK, h=4, i=2)[:, t],
            )

        def quantize(pool, values, name):
            width = values.shape[1] // PACK
            codes = pool.tile([P, width], U32, name=name + "_codes", align_bytes=64)
            scales = pool.tile([P, width], U8, name=name + "_scales", align_bytes=64)
            nc.vector.quantize_mx(out=codes[:].bitcast(FP8X4), scales=scales[:], in_=values)
            return codes, scales

        def product(dst, weights, col, words, scales):
            nc.tensor.matmul_mx(
                out=dst,
                lhsT=weights[0][:, col : col + P].bitcast(FP8X4),
                lhsT_scale=weights[1][:, col : col + P],
                rhs=words.bitcast(FP8X4),
                rhs_scale=scales,
                start=True,
                stop=True,
            )

        def project(weights, col, parts, name):
            bank = psum.tile([P, S], F32, name="bank")
            at = 0
            for words, scales in parts:
                product(bank[:, at : at + words.shape[1]], weights, col, words, scales)
                at = at + words.shape[1]
            res = keep.tile([P, at], F32, name=name)
            nc.scalar.copy(res[:], bank[:, :at])
            return res

        def scatter(window, lst, values, lo, hi):
            nc.vector.tensor_copy(window[:].indirect(lst[:, lo // LIST_ROWS : hi // LIST_ROWS]), values[:])

        offs_scales = gather_scales(offs_t, "offs_scales")
        two_scales = gather_scales(two_t, "two_scales")
        half = S // 2
        offs_words = gather_words(offs_t, 0, S, "offs_words", "offs_words")
        two_lo = gather_words(two_t, 0, half, "two_lo", "two_lo")
        w1_bf = []
        for t in range(PACK):
            dealt = keep.tile([P, P * PACK], BF16, name="w1_bf", tag="w1_bf" + str(t), align_bytes=64)
            deal_weight(nc.vector.tensor_copy if t < 2 else nc.scalar.copy, dealt[:], w1_raw, t)
            w1_bf.append(dealt)
        w1_q = [quantize(keep, w1_bf[t][:], "w1_" + str(t)) for t in range(2)]
        two_hi = gather_words(two_t, half, S, "two_hi", "w1_bf0")
        w1_q = w1_q + [quantize(keep, w1_bf[t][:], "w1_" + str(t)) for t in range(2, PACK)]
        offs_all = [(offs_words[:], offs_scales[:])]
        two_all = [(two_lo[:], two_scales[:, :half]), (two_hi[:], two_scales[:, half:])]
        y0a = project(w1_q[0], 0, [(offs_words[:, :half], offs_scales[:, :half])], "y0a")
        y1 = project(w1_q[1], 0, offs_all, "y1")
        y0b = project(w1_q[0], 0, [(offs_words[:, half:], offs_scales[:, half:])], "y0b")
        y2 = project(w1_q[2], 0, offs_all, "y2")
        y3 = project(w1_q[3], 0, offs_all, "y3")

        merged = [keep.tile([P, U], F32, name="merged" + str(t), align_bytes=64) for t in range(PACK - 1)]
        scatter(merged[0], la_t, y0a, 0, S // 2)
        scatter(merged[1], la_t, y1, 0, S)
        scatter(merged[0], la_t, y0b, S // 2, S)
        scatter(merged[2], la_t, y2, 0, S)

        w2_bf = keep.tile([P, H * PACK], BF16, name="w2_bf", align_bytes=64)
        for t in range(PACK):
            deal_weight(nc.scalar.copy, w2_bf[:, t * P * PACK : (t + 1) * P * PACK], w2_raw, t)
        w2_q = quantize(keep, w2_bf[:], "w2")
        merged.append(keep.tile([P, U], F32, name="merged3", tag="w2_raw", align_bytes=64))
        scatter(merged[3], la_t, y3, 0, S)
        e = [project(w2_q, t * P, two_all, "e" + str(t)) for t in range(PACK)]

        w3_bf = keep.tile([P, N * PACK], BF16, name="w3_bf", tag="w3_bf", align_bytes=64)
        nc.scalar.copy(
            w3_bf[:].rearrange("p (c i j) -> p c j i", i=2, j=PACK),
            w3_raw[:].rearrange("p j (c i) -> p c j i", i=2),
        )
        w3_q = quantize(keep, w3_bf[:], "w3")

        joined = keep.tile([P, PACK, U], F32, name="joined", tag="w3_bf", align_bytes=64)
        for t in range(PACK):
            scatter(merged[t], lb_t, e[t], 0, S)
            nc.scalar.copy(joined[:, t, :], merged[t][:])

        out_view = out.rearrange("(b p) w -> p b w", p=P)
        for spans, pieces, slot in STAGES:
            lo, hi = spans[0][0], spans[-1][1]
            mates = keep.tile([P, PACK, hi - lo], F32, name="mates", tag=slot, align_bytes=64)
            for a, b in spans:
                for t in range(PACK):
                    nc.vector.tensor_copy(
                        mates[:, t, a - lo : b - lo],
                        merged[t][:].indirect(mate_t[:, a // LIST_ROWS : b // LIST_ROWS]),
                    )
            zs = []
            for a, b in pieces:
                z = keep.tile([P, (b - a) * PACK], BF16, name="z", tag="z" + str(a), align_bytes=64)
                nc.vector.tensor_tensor(
                    z[:].rearrange("p (c i t) -> p c t i", i=2, t=PACK),
                    joined[:, :, a:b].rearrange("p t (c i) -> p c t i", i=2),
                    mates[:, :, a - lo : b - lo].rearrange("p t (c i) -> p c t i", i=2),
                    MAX,
                )
                zs.append(z)
            for (a, b), z in zip(pieces, zs):
                width = b - a
                z_q = quantize(keep, z[:], "z" + str(a))
                per_bank = 2 if b == U else S // width
                for first_block in range(0, PACK, per_bank):
                    bank = psum.tile([P, S], F32, name="bank")
                    for i in range(per_bank):
                        product(bank[:, i * width : (i + 1) * width], w3_q, (first_block + i) * P, z_q[0][:], z_q[1][:])
                    staged = ring.tile([P, per_bank * width], F32, name="staged", bufs=9)
                    copy = nc.vector.tensor_copy if b == U and first_block == 0 else nc.scalar.copy
                    copy(staged[:], bank[:, : per_bank * width])
                    nc.sync.dma_start(
                        out_view[:, first_block : first_block + per_bank, a:b],
                        staged[:].rearrange("p (b w) -> p b w", b=per_bank),
                    )
